import numpy as np
import ml_dtypes


def mxq(x, axis, fmt="e4m3"):
    dtype, down = {"e4m3": (ml_dtypes.float8_e4m3fn, 7), "e5m2": (ml_dtypes.float8_e5m2, 14)}[fmt]
    v = np.moveaxis(np.asarray(x, np.float32).astype(ml_dtypes.bfloat16).astype(np.float64), axis, -1)
    blocks = v.reshape(v.shape[:-1] + (-1, 32))
    amax = np.abs(blocks).max(-1, keepdims=True)
    byte = np.maximum(np.where(amax > 0, np.frexp(amax)[1] - 1 + 127, 0) - down, 1)
    scale = np.exp2(byte - 127.0)
    codes = (blocks / scale).astype(np.float32).astype(dtype).astype(np.float64)
    return np.moveaxis((codes * scale).reshape(v.shape), -1, axis)


WIDE = False


def mx_kscale(k):
    if not WIDE:
        return np.ones(k)
    levels = np.array([10, -10, 5, -5, 0])
    if k % 512:
        return np.exp2(np.random.permutation(np.resize(levels, k // 32))).repeat(32)
    a = np.empty((k // 512, 16))
    for p in range(k // 512):
        a[p, :8] = np.random.permutation(np.resize(levels, 8))
        for g in range(8):
            far = levels[np.abs(levels - a[p, g]) >= 10]
            a[p, g + 8] = far[np.random.randint(len(far))]
    return np.exp2(a.ravel()).repeat(32)


def f64(x):
    return np.asarray(x).astype(np.float64)


def striped(idx):
    return np.tile(idx.reshape(-1, 16).T, (8, 1)).astype(np.uint16)


def unstriped(offs):
    return offs[:16].T.reshape(-1).astype(np.int64)


E2M1 = np.array([0.0, 0.5, 1.0, 1.5, 2.0, 3.0, 4.0, 6.0, -0.0, -0.5, -1.0, -1.5, -2.0, -3.0, -4.0, -6.0])


def pack_weight(w, fmt):
    k, n = w.shape
    w = f64(np.asarray(w, np.float32).astype(ml_dtypes.bfloat16)).reshape(k // 32, 32, n)
    amax = np.abs(w).max(1)
    if fmt == "e4m3":
        byte = np.frexp(amax)[1] - 1 + 127 - 7
    else:
        mant, ex = np.frexp(amax / 6.0)
        byte = np.where(mant > 0.5, ex, ex - 1) + 127
    byte = np.clip(np.where(amax > 0, byte, 1), 1, 254)
    scaled = (w * np.exp2(127.0 - byte)[:, None, :]).reshape(k, n).astype(np.float32)
    by_word = np.ascontiguousarray(scaled.reshape(k // 512, 128, 4, n).transpose(0, 1, 3, 2))
    if fmt == "e4m3":
        words = by_word.astype(ml_dtypes.float8_e4m3fn).view(np.uint8)
    else:
        c = by_word.astype(ml_dtypes.float4_e2m1fn).view(np.uint8) & 0xF
        words = (c[..., 0::2] | (c[..., 1::2] << 4)).reshape(k // 512, 128, 2 * n)
    return np.ascontiguousarray(words), np.ascontiguousarray(byte.astype(np.uint8).reshape(k // 512, 16, n))


def unpack_weight(words, scales, fmt):
    g, _, n = scales.shape
    words = np.ascontiguousarray(words).reshape(g, 128, n, -1)
    if fmt == "e4m3":
        vals = words.view(ml_dtypes.float8_e4m3fn).astype(np.float64)
    else:
        nib = np.empty((g, 128, n, 4), np.uint8)
        nib[..., 0::2] = words & 0xF
        nib[..., 1::2] = words >> 4
        vals = E2M1[nib]
    vals = vals * np.repeat(np.exp2(scales.astype(np.float64) - 127.0), 8, axis=1)[..., None]
    return vals.transpose(0, 1, 3, 2).reshape(g * 512, n)


def gelu(v):
    return 0.5 * v * (1.0 + np.tanh(np.sqrt(2.0 / np.pi) * (v + 0.044715 * v**3)))


K, T, S, H, S2, T3, T2 = 1024, 4096, 1024, 512, 512, 2048, 2048

def setup_inputs():
    n = np.random.standard_normal
    s = mx_kscale(K)[:, None]
    u = mx_kscale(H)[:, None]
    tab_words, tab_scales = pack_weight(n((K, T)) * s, "e4m3")
    tab2_words, tab2_scales = pack_weight(n((H, T3)) / np.sqrt(H) / u, "e4m3")
    w2_words, w2_scales = pack_weight(n((K, H)) / np.sqrt(K) / s * u.T, "e2m1")
    w4_words, w4_scales = pack_weight(n((K, S2)) / np.sqrt(K) / s, "e4m3")
    return {
        "tab_words": tab_words, "tab_scales": tab_scales,
        "tab2_words": tab2_words, "tab2_scales": tab2_scales,
        "offs": striped(np.random.permutation(T)[:S]),
        "offs2": striped(np.random.permutation(T3)[:S2]),
        "offs3": striped(np.random.permutation(T2)[:S]),
        "w1": (n((K, H)) / np.sqrt(K) / s * u.T).astype(np.float32),
        "w2_words": w2_words, "w2_scales": w2_scales,
        "w3": (1.3 * n((K, H)) / np.sqrt(K) / s).astype(np.float32),
        "b": (0.7 * n(H)).astype(np.float32),
        "gain": (1.2 * np.exp(0.3 * n(H)) * u[:, 0]).astype(np.float32),
        "w4_words": w4_words, "w4_scales": w4_scales,
        "d": np.exp(0.4 * n(S2)).astype(np.float32),
        "jury": n((S2, S)).astype(np.float32),
        "page1": n((S2, T2)).astype(np.float32),
        "wgo": np.exp(0.3 * n((128, S))).astype(np.float32),
    }

def reference(tab_words, tab_scales, tab2_words, tab2_scales, offs, offs2, offs3, w1, w2_words, w2_scales, w3, b, gain, w4_words, w4_scales, d, jury, page1, wgo):
    v = unpack_weight(tab_words, tab_scales, "e4m3")[:, unstriped(offs)]
    v2 = unpack_weight(tab2_words, tab2_scales, "e4m3")[:, unstriped(offs2)]
    w2 = unpack_weight(w2_words, w2_scales, "e2m1")
    w4 = unpack_weight(w4_words, w4_scales, "e4m3")
    f1 = mxq(f64(w1), 0, "e4m3").T @ v
    f2 = w2.T @ v
    f3 = mxq(f64(w3), 0, "e4m3").T @ v
    h = np.maximum(f1, f2) + f64(gain)[:, None] * np.tanh(f3 + f64(b)[:, None])
    hq = mxq(h, 0, "e4m3")
    e = v2.T @ hq + w4.T @ v
    y = f64(d)[:, None] * e + f64(jury)
    out = f64(page1).copy()
    out[:, unstriped(offs3)] = np.tile(f64(wgo), (S2 // 128, 1)) * y
    return out

@@ -1,0 +1,286 @@
+from contextlib import ExitStack
+
+import concourse.mybir as mybir
+from concourse.masks import make_identity
+
+K, T, S, H, S2, T3, T2 = 1024, 4096, 1024, 512, 512, 2048, 2048
+FLOPS = 2 * S * (3 * K * H + H * S2 + K * S2)
+
+F32 = mybir.dt.float32
+BF16 = mybir.dt.bfloat16
+I32 = mybir.dt.int32
+U32 = mybir.dt.uint32
+U16 = mybir.dt.uint16
+U8 = mybir.dt.uint8
+FP8X4 = mybir.dt.float8_e4m3fn_x4
+FP4X4 = mybir.dt.float4_e2m1fn_x4
+ALU = mybir.AluOpType
+ACT = mybir.ActivationFunctionType
+
+P = 128
+PACK = 4
+K_PASS = P * PACK
+PASSES = K // K_PASS
+QUADS = 4
+HALF = 512
+HALVES = S // HALF
+LIST_COLS = HALF // 16
+ROW_TILES = S2 // P
+VECTOR_SHARE = 80
+
+
+def tile_list_laureate_shortlist_page_kernel(
+    tc, tab_words, tab_scales, tab2_words, tab2_scales, offs, offs2, offs3, w1, w2_words, w2_scales,
+    w3, b, gain, w4_words, w4_scales, d, jury, page1, wgo, out,
+):
+    nc = tc.nc
+    with ExitStack() as ctx:
+        keep = ctx.enter_context(tc.tile_pool(name="keep", bufs=1))
+        ring = ctx.enter_context(tc.tile_pool(name="ring", bufs=2))
+        psum = ctx.enter_context(tc.psum_pool(name="psum", bufs=2))
+
+        def kept(shape, dtype, name):
+            return keep.tile(shape, dtype, name=name, align_bytes=64)
+
+        def load_scale_rows(tile, src, queue):
+            nc.vector.memset(tile[:].bitcast(I32), 0)
+            passes = src.shape[0]
+            for q in range(QUADS):
+                queue.dma_start(
+                    out=tile[32 * q : 32 * q + 4, :].bitcast(I32).rearrange("r (a c) -> r a c", a=passes),
+                    in_=src[:, 4 * q : 4 * q + 4, :].rearrange("a r c -> r a c").bitcast(I32),
+                )
+
+        def load_words(tile, src):
+            nc.sync.dma_start(out=tile[:].bitcast(I32), in_=src.rearrange("p t i -> p (t i)").bitcast(I32))
+
+        def load_weight(w, a, name):
+            raw = kept([P, PACK, H], F32, name)
+            nc.sync.dma_start(out=raw[:], in_=w[a * K_PASS : (a + 1) * K_PASS, :].rearrange("(p j) c -> p j c", j=PACK))
+            return raw
+
+        idx = kept([P, S // 16], U16, "idx")
+        idx2 = kept([P, S2 // 16], U16, "idx2")
+        idx3 = kept([P, S // 16], U16, "idx3")
+        nc.sync.dma_start(idx[:], offs)
+
+        tab_sc = kept([P, PASSES * T], U8, "tab_sc")
+        load_scale_rows(tab_sc, tab_scales, nc.gpsimd)
+        w2_sc_raw = kept([P, PASSES * H], U8, "w2_sc_raw")
+        load_scale_rows(w2_sc_raw, w2_scales, nc.gpsimd)
+        tab2_sc = kept([P, T3], U8, "tab2_sc")
+        load_scale_rows(tab2_sc, tab2_scales, nc.gpsimd)
+        w4_sc = kept([P, PASSES * S2], U8, "w4_sc")
+        load_scale_rows(w4_sc, w4_scales, nc.gpsimd)
+        ident = kept([P, P], F32, "ident")
+        make_identity(nc, ident[:])
+
+        tab_w = [kept([P, T], U32, f"tab_w{a}") for a in range(PASSES)]
+        load_words(tab_w[0], tab_words[0])
+
+        w2_raw = kept([P, PASSES * 2 * H], U8, "w2_raw")
+        nc.sync.dma_start(
+            out=w2_raw[:].bitcast(I32).rearrange("p (a c) -> p a c", a=PASSES),
+            in_=w2_words.rearrange("a p c -> p a c").bitcast(I32),
+        )
+        w1_raw = [load_weight(w1, 0, "w1_raw0")]
+        load_words(tab_w[1], tab_words[1])
+        nc.sync.dma_start(idx2[:], offs2)
+        w1_raw.append(load_weight(w1, 1, "w1_raw1"))
+        w3_raw = [load_weight(w3, a, f"w3_raw{a}") for a in range(PASSES)]
+        b_sb = kept([P, PACK], F32, "b_sb")
+        nc.sync.dma_start(out=b_sb[:], in_=b.rearrange("(p t) -> p t", t=PACK))
+        gain_sb = kept([P, PACK], F32, "gain_sb")
+        nc.sync.dma_start(out=gain_sb[:], in_=gain.rearrange("(p t) -> p t", t=PACK))
+        tab2_w = kept([P, T3], U32, "tab2_w")
+        load_words(tab2_w, tab2_words[0])
+        w4_w = kept([P, PASSES * S2], U32, "w4_w")
+        nc.sync.dma_start(
+            out=w4_w[:].bitcast(I32).rearrange("p (a c) -> p a c", a=PASSES),
+            in_=w4_words.rearrange("a p c i -> p a (c i)").bitcast(I32),
+        )
+        d_sb = kept([P, ROW_TILES], F32, "d_sb")
+        with nc.allow_non_contiguous_dma(reason="one value of d for each partition and row tile"):
+            nc.sync.dma_start(out=d_sb[:], in_=d.rearrange("(c p) -> p c", p=P))
+        nc.sync.dma_start(idx3[:], offs3)
+
+        wgo_sb, jury_sb, page = {}, {}, {}
+
+        def load_wgo(hf):
+            wgo_sb[hf] = kept([P, HALF], F32, f"wgo{hf}")
+            nc.sync.dma_start(out=wgo_sb[hf][:], in_=wgo[:, hf * HALF : (hf + 1) * HALF])
+
+        def load_jury(c, hf):
+            jury_sb[c, hf] = kept([P, HALF], F32, f"jury{c}_{hf}")
+            nc.sync.dma_start(out=jury_sb[c, hf][:], in_=jury[c * P : (c + 1) * P, hf * HALF : (hf + 1) * HALF])
+
+        def load_page(c):
+            page[c] = kept([P, T2], F32, f"page{c}")
+            nc.sync.dma_start(out=page[c][:], in_=page1[c * P : (c + 1) * P, :])
+
+        load_wgo(0)
+        for c in range(ROW_TILES):
+            load_jury(c, 0)
+            load_page(c)
+        load_wgo(1)
+        for c in range(ROW_TILES):
+            load_jury(c, 1)
+
+        w2_w = kept([P, PASSES * 2 * H], U8, "w2_w")
+        nc.vector.tensor_copy(
+            out=w2_w[:].bitcast(U16).rearrange("p (a t m) -> p a t m", a=PASSES, t=PACK),
+            in_=w2_raw[:].bitcast(U16).rearrange("p (a m t) -> p a t m", a=PASSES, t=PACK),
+        )
+
+        v_w = [kept([P, S], U32, f"v_w{a}") for a in range(PASSES)]
+        v_sc = [kept([P, S], U8, f"v_sc{a}") for a in range(PASSES)]
+        for a in range(PASSES):
+            nc.vector.tensor_copy(v_sc[a][:], tab_sc[:, a * T : (a + 1) * T].indirect(idx[:]))
+        nc.vector.tensor_copy(v_w[0][:], tab_w[0][:].indirect(idx[:]))
+
+        w2_sc = kept([P, PASSES * H], U8, "w2_sc")
+        nc.vector.tensor_copy(
+            out=w2_sc[:].rearrange("p (a t m) -> p a t m", a=PASSES, t=PACK),
+            in_=w2_sc_raw[:].rearrange("p (a m t) -> p a t m", a=PASSES, t=PACK),
+        )
+
+        def quantize_weight(raw, name, split):
+            grouped = ring.tile([P, PACK * H], BF16, name="grouped", align_bytes=64)
+            dst = grouped[:].rearrange("p (t m j) -> p m j t", t=PACK, j=PACK)
+            src = raw[:].rearrange("p j (m t) -> p m j t", t=PACK)
+            if split:
+                nc.vector.tensor_copy(out=dst[:, :split], in_=src[:, :split])
+            if split < P:
+                nc.scalar.copy(out=dst[:, split:], in_=src[:, split:])
+            codes = kept([P, H], U32, name + "_w")
+            scales = kept([P, H], U8, name + "_sc")
+            nc.vector.quantize_mx(out=codes[:].bitcast(FP8X4), scales=scales[:], in_=grouped[:])
+            return codes, scales
+
+        w1_q = [quantize_weight(w1_raw[0], "w1q0", 0)]
+
+        for hf in range(HALVES):
+            nc.vector.tensor_copy(
+                v_w[1][:, hf * HALF : (hf + 1) * HALF],
+                tab_w[1][:].indirect(idx[:, hf * LIST_COLS : (hf + 1) * LIST_COLS]),
+            )
+
+        v2_sc = kept([P, S2], U8, "v2_sc")
+        nc.vector.tensor_copy(v2_sc[:], tab2_sc[:].indirect(idx2[:]))
+
+        def product(acc, stationary, hf, start=True, stop=True):
+            cols = slice(hf * HALF, (hf + 1) * HALF)
+            for a in range(PASSES):
+                lhs, lhs_sc = stationary[a]
+                nc.tensor.matmul_mx(
+                    out=acc[:], lhsT=lhs, lhsT_scale=lhs_sc,
+                    rhs=v_w[a][:, cols].bitcast(FP8X4), rhs_scale=v_sc[a][:, cols],
+                    start=start and a == 0, stop=stop and a == PASSES - 1,
+                )
+
+        def columns(q, t):
+            return [(codes[:, t * P : (t + 1) * P].bitcast(FP8X4), scales[:, t * P : (t + 1) * P]) for codes, scales in q]
+
+        best = {}
+
+        def second_feature(hf, store):
+            for t in range(PACK):
+                acc = psum.tile([P, HALF], F32, name="f", bufs=3)
+                stationary = [
+                    (
+                        w2_w[:, 2 * (a * H + t * P) : 2 * (a * H + (t + 1) * P)].bitcast(FP4X4),
+                        w2_sc[:, a * H + t * P : a * H + (t + 1) * P],
+                    )
+                    for a in range(PASSES)
+                ]
+                product(acc, stationary, hf)
+                best[hf, t] = store[:, t, :]
+                nc.scalar.copy(out=best[hf, t], in_=acc[:])
+
+        def first_feature(hf):
+            for t in range(PACK):
+                acc = psum.tile([P, HALF], F32, name="f", bufs=3)
+                product(acc, columns(w1_q, t), hf)
+                nc.vector.tensor_tensor(out=best[hf, t], in0=acc[:], in1=best[hf, t], op=ALU.max)
+
+        h_q = {}
+
+        def features(hf, weave):
+            planes = ring.tile([P, PACK * HALF], BF16, name="planes", align_bytes=64)
+            for t in range(PACK):
+                acc = psum.tile([P, HALF], F32, name="f", bufs=3)
+                product(acc, columns(w3_q, t), hf)
+                th = ring.tile([P, HALF], F32, name="th", bufs=3)
+                nc.scalar.activation(out=th[:], in_=acc[:], func=ACT.Tanh, bias=b_sb[:, t : t + 1])
+                nc.vector.scalar_tensor_tensor(
+                    out=planes[:, t * HALF : (t + 1) * HALF], in0=th[:], scalar=gain_sb[:, t : t + 1],
+                    in1=best[hf, t], op0=ALU.mult, op1=ALU.add,
+                )
+            woven = ring.tile([P, HALF * PACK], BF16, name="woven", align_bytes=64)
+            weave(
+                out=woven[:].rearrange("p (c i t) -> p c t i", i=4, t=PACK),
+                in_=planes[:].rearrange("p (t c i) -> p c t i", t=PACK, i=4),
+            )
+            codes = kept([P, HALF], U32, f"h_w{hf}")
+            scales = kept([P, HALF], U8, f"h_sc{hf}")
+            nc.vector.quantize_mx(out=codes[:].bitcast(FP8X4), scales=scales[:], in_=woven[:])
+            h_q[hf] = codes, scales
+
+        def scores(c, hf, on_vector=False):
+            acc = psum.tile([P, HALF], F32, name="e")
+            stationary = [
+                (
+                    w4_w[:, a * S2 + c * P : a * S2 + (c + 1) * P].bitcast(FP8X4),
+                    w4_sc[:, a * S2 + c * P : a * S2 + (c + 1) * P],
+                )
+                for a in range(PASSES)
+            ]
+            product(acc, stationary, hf, stop=False)
+            codes, scales = h_q[hf]
+            nc.tensor.matmul_mx(
+                out=acc[:], lhsT=v2_w[:, c * P : (c + 1) * P].bitcast(FP8X4), lhsT_scale=v2_sc[:, c * P : (c + 1) * P],
+                rhs=codes[:].bitcast(FP8X4), rhs_scale=scales[:], start=False, stop=True,
+            )
+            y = ring.tile([P, HALF], F32, name="y", bufs=3)
+            if on_vector:
+                nc.vector.scalar_tensor_tensor(
+                    out=y[:], in0=acc[:], scalar=d_sb[:, c : c + 1], in1=jury_sb[c, hf][:], op0=ALU.mult, op1=ALU.add,
+                )
+            else:
+                z = ring.tile([P, HALF], F32, name="z")
+                nc.scalar.activation(out=z[:], in_=acc[:], func=ACT.Copy, scale=d_sb[:, c : c + 1])
+                turned = psum.tile([P, HALF], F32, name="turned")
+                blocks = [slice(i * P, (i + 1) * P) for i in range(HALF // P)]
+                for n, term in enumerate((jury_sb[c, hf], z)):
+                    for i, blk in enumerate(blocks):
+                        nc.tensor.matmul(
+                            turned[:, blk], term[:, blk], ident[:], is_transpose=True,
+                            start=(n == 0 and i == 0), stop=(n == 1 and i == len(blocks) - 1),
+                        )
+                y_t = ring.tile([P, HALF], F32, name="y_t")
+                nc.scalar.copy(out=y_t[:], in_=turned[:])
+                back = psum.tile([P, HALF], F32, name="back", bufs=1)
+                for blk in blocks:
+                    nc.tensor.transpose(back[:, blk], y_t[:, blk], ident[:])
+                nc.scalar.copy(out=y[:], in_=back[:])
+            nc.vector.tensor_tensor(
+                page[c][:].indirect(idx3[:, hf * LIST_COLS : (hf + 1) * LIST_COLS]), y[:], wgo_sb[hf][:], ALU.mult,
+            )
+
+        second_feature(0, kept([P, PACK, HALF], F32, "best0"))
+        w1_q.append(quantize_weight(w1_raw[1], "w1q1", P))
+        first_feature(0)
+        w3_q = [quantize_weight(w3_raw[0], "w3q0", 0), quantize_weight(w3_raw[1], "w3q1", VECTOR_SHARE)]
+        features(0, nc.vector.tensor_copy)
+        v2_w = kept([P, S2], U32, "v2_w")
+        nc.vector.tensor_copy(v2_w[:], tab2_w[:].indirect(idx2[:]))
+        second_feature(1, kept([P, PACK, HALF], F32, "w3_raw1"))
+        first_feature(1)
+        scores(0, 0, on_vector=True)
+        scores(1, 0)
+        features(1, nc.scalar.copy)
+        scores(2, 0)
+        scores(3, 0)
+        for c in range(ROW_TILES):
+            scores(c, 1)
+            nc.sync.dma_start(out=out[c * P : (c + 1) * P, :], in_=page[c][:])

@@ -42,11 +42,10 @@ def tile_list_laureate_shortlist_page_kernel(
         def kept(shape, dtype, name):
             return keep.tile(shape, dtype, name=name, align_bytes=64)
 
-        def load_scale_rows(tile, src, queue):
-            nc.vector.memset(tile[:].bitcast(I32), 0)
+        def load_scale_rows(tile, src):
             passes = src.shape[0]
             for q in range(QUADS):
-                queue.dma_start(
+                nc.sync.dma_start(
                     out=tile[32 * q : 32 * q + 4, :].bitcast(I32).rearrange("r (a c) -> r a c", a=passes),
                     in_=src[:, 4 * q : 4 * q + 4, :].rearrange("a r c -> r a c").bitcast(I32),
                 )
@@ -59,50 +58,51 @@ def tile_list_laureate_shortlist_page_kernel(
             nc.sync.dma_start(out=raw[:], in_=w[a * K_PASS : (a + 1) * K_PASS, :].rearrange("(p j) c -> p j c", j=PACK))
             return raw
 
+        tab_sc = kept([P, PASSES * T], U8, "tab_sc")
+        nc.vector.memset(tab_sc[:, :T].bitcast(I32), 0)
+        nc.gpsimd.memset(tab_sc[:, T:].bitcast(I32), 0)
+        w2_sc_raw = kept([P, PASSES * H], U8, "w2_sc_raw")
+        tab2_sc = kept([P, T3], U8, "tab2_sc")
+        w4_sc = kept([P, PASSES * S2], U8, "w4_sc")
+        for tile in (w2_sc_raw, tab2_sc, w4_sc):
+            nc.vector.memset(tile[:].bitcast(I32), 0)
+        ident = kept([P, P], F32, "ident")
+        make_identity(nc, ident[:])
+
         idx = kept([P, S // 16], U16, "idx")
         idx2 = kept([P, S2 // 16], U16, "idx2")
         idx3 = kept([P, S // 16], U16, "idx3")
         nc.sync.dma_start(idx[:], offs)
-
-        tab_sc = kept([P, PASSES * T], U8, "tab_sc")
-        load_scale_rows(tab_sc, tab_scales, nc.gpsimd)
-        w2_sc_raw = kept([P, PASSES * H], U8, "w2_sc_raw")
-        load_scale_rows(w2_sc_raw, w2_scales, nc.gpsimd)
-        tab2_sc = kept([P, T3], U8, "tab2_sc")
-        load_scale_rows(tab2_sc, tab2_scales, nc.gpsimd)
-        w4_sc = kept([P, PASSES * S2], U8, "w4_sc")
-        load_scale_rows(w4_sc, w4_scales, nc.gpsimd)
-        ident = kept([P, P], F32, "ident")
-        make_identity(nc, ident[:])
-
-        tab_w = [kept([P, T], U32, f"tab_w{a}") for a in range(PASSES)]
-        load_words(tab_w[0], tab_words[0])
-
-        w2_raw = kept([P, PASSES * 2 * H], U8, "w2_raw")
-        nc.sync.dma_start(
-            out=w2_raw[:].bitcast(I32).rearrange("p (a c) -> p a c", a=PASSES),
-            in_=w2_words.rearrange("a p c -> p a c").bitcast(I32),
-        )
-        w1_raw = [load_weight(w1, 0, "w1_raw0")]
-        load_words(tab_w[1], tab_words[1])
         nc.sync.dma_start(idx2[:], offs2)
-        w1_raw.append(load_weight(w1, 1, "w1_raw1"))
-        w3_raw = [load_weight(w3, a, f"w3_raw{a}") for a in range(PASSES)]
+        nc.sync.dma_start(idx3[:], offs3)
         b_sb = kept([P, PACK], F32, "b_sb")
         nc.sync.dma_start(out=b_sb[:], in_=b.rearrange("(p t) -> p t", t=PACK))
         gain_sb = kept([P, PACK], F32, "gain_sb")
         nc.sync.dma_start(out=gain_sb[:], in_=gain.rearrange("(p t) -> p t", t=PACK))
+        w2_raw = kept([P, PASSES * 2 * H], U8, "w2_raw")
+        for a in range(PASSES):
+            nc.sync.dma_start(out=w2_raw[:, 2 * H * a : 2 * H * (a + 1)].bitcast(I32), in_=w2_words[a].bitcast(I32))
+        tab_w = [kept([P, T], U32, f"tab_w{a}") for a in range(PASSES)]
+        load_words(tab_w[0], tab_words[0])
+        load_scale_rows(tab_sc, tab_scales)
+        w1_raw = [load_weight(w1, 0, "w1_raw0")]
+        load_scale_rows(w2_sc_raw, w2_scales)
+        w3_raw = [load_weight(w3, 0, "w3_raw0")]
+        load_words(tab_w[1], tab_words[1])
+        w1_raw.append(load_weight(w1, 1, "w1_raw1"))
+        w3_raw.append(load_weight(w3, 1, "w3_raw1"))
+        d_sb = kept([P, ROW_TILES], F32, "d_sb")
+        with nc.allow_non_contiguous_dma(reason="one value of d for each partition and row tile"):
+            nc.sync.dma_start(out=d_sb[:], in_=d.rearrange("(c p) -> p c", p=P))
+        load_scale_rows(tab2_sc, tab2_scales)
         tab2_w = kept([P, T3], U32, "tab2_w")
         load_words(tab2_w, tab2_words[0])
+        load_scale_rows(w4_sc, w4_scales)
         w4_w = kept([P, PASSES * S2], U32, "w4_w")
         nc.sync.dma_start(
             out=w4_w[:].bitcast(I32).rearrange("p (a c) -> p a c", a=PASSES),
             in_=w4_words.rearrange("a p c i -> p a (c i)").bitcast(I32),
         )
-        d_sb = kept([P, ROW_TILES], F32, "d_sb")
-        with nc.allow_non_contiguous_dma(reason="one value of d for each partition and row tile"):
-            nc.sync.dma_start(out=d_sb[:], in_=d.rearrange("(c p) -> p c", p=P))
-        nc.sync.dma_start(idx3[:], offs3)
 
         wgo_sb, jury_sb, page = {}, {}, {}
 
@@ -134,9 +134,9 @@ def tile_list_laureate_shortlist_page_kernel(
 
         v_w = [kept([P, S], U32, f"v_w{a}") for a in range(PASSES)]
         v_sc = [kept([P, S], U8, f"v_sc{a}") for a in range(PASSES)]
+        nc.vector.tensor_copy(v_w[0][:], tab_w[0][:].indirect(idx[:]))
         for a in range(PASSES):
             nc.vector.tensor_copy(v_sc[a][:], tab_sc[:, a * T : (a + 1) * T].indirect(idx[:]))
-        nc.vector.tensor_copy(v_w[0][:], tab_w[0][:].indirect(idx[:]))
 
         w2_sc = kept([P, PASSES * H], U8, "w2_sc")
         nc.vector.tensor_copy(
@@ -158,15 +158,13 @@ def tile_list_laureate_shortlist_page_kernel(
             return codes, scales
 
         w1_q = [quantize_weight(w1_raw[0], "w1q0", 0)]
+        w3_q = [quantize_weight(w3_raw[0], "w3q0", 0)]
 
         for hf in range(HALVES):
             nc.vector.tensor_copy(
                 v_w[1][:, hf * HALF : (hf + 1) * HALF],
                 tab_w[1][:].indirect(idx[:, hf * LIST_COLS : (hf + 1) * LIST_COLS]),
             )
-
-        v2_sc = kept([P, S2], U8, "v2_sc")
-        nc.vector.tensor_copy(v2_sc[:], tab2_sc[:].indirect(idx2[:]))
 
         def product(acc, stationary, hf, start=True, stop=True):
             cols = slice(hf * HALF, (hf + 1) * HALF)
@@ -185,7 +183,7 @@ def tile_list_laureate_shortlist_page_kernel(
 
         def second_feature(hf, store):
             for t in range(PACK):
-                acc = psum.tile([P, HALF], F32, name="f", bufs=3)
+                acc = psum.tile([P, HALF], F32, name="bank_a")
                 stationary = [
                     (
                         w2_w[:, 2 * (a * H + t * P) : 2 * (a * H + (t + 1) * P)].bitcast(FP4X4),
@@ -197,18 +195,21 @@ def tile_list_laureate_shortlist_page_kernel(
                 best[hf, t] = store[:, t, :]
                 nc.scalar.copy(out=best[hf, t], in_=acc[:])
 
-        def first_feature(hf):
+        def first_feature(hf, store=None):
             for t in range(PACK):
-                acc = psum.tile([P, HALF], F32, name="f", bufs=3)
+                acc = psum.tile([P, HALF], F32, name="bank_b")
                 product(acc, columns(w1_q, t), hf)
-                nc.vector.tensor_tensor(out=best[hf, t], in0=acc[:], in1=best[hf, t], op=ALU.max)
+                f2 = best[hf, t]
+                if store is not None:
+                    best[hf, t] = store[:, t, :]
+                nc.vector.tensor_tensor(out=best[hf, t], in0=acc[:], in1=f2, op=ALU.max)
 
         h_q = {}
 
         def features(hf, weave):
             planes = ring.tile([P, PACK * HALF], BF16, name="planes", align_bytes=64)
             for t in range(PACK):
-                acc = psum.tile([P, HALF], F32, name="f", bufs=3)
+                acc = psum.tile([P, HALF], F32, name="bank_c")
                 product(acc, columns(w3_q, t), hf)
                 th = ring.tile([P, HALF], F32, name="th", bufs=3)
                 nc.scalar.activation(out=th[:], in_=acc[:], func=ACT.Tanh, bias=b_sb[:, t : t + 1])
@@ -249,7 +250,7 @@ def tile_list_laureate_shortlist_page_kernel(
             else:
                 z = ring.tile([P, HALF], F32, name="z")
                 nc.scalar.activation(out=z[:], in_=acc[:], func=ACT.Copy, scale=d_sb[:, c : c + 1])
-                turned = psum.tile([P, HALF], F32, name="turned")
+                turned = psum.tile([P, HALF], F32, name="bank_a")
                 blocks = [slice(i * P, (i + 1) * P) for i in range(HALF // P)]
                 for n, term in enumerate((jury_sb[c, hf], z)):
                     for i, blk in enumerate(blocks):
@@ -259,7 +260,7 @@ def tile_list_laureate_shortlist_page_kernel(
                         )
                 y_t = ring.tile([P, HALF], F32, name="y_t")
                 nc.scalar.copy(out=y_t[:], in_=turned[:])
-                back = psum.tile([P, HALF], F32, name="back", bufs=1)
+                back = psum.tile([P, HALF], F32, name="bank_b")
                 for blk in blocks:
                     nc.tensor.transpose(back[:, blk], y_t[:, blk], ident[:])
                 nc.scalar.copy(out=y[:], in_=back[:])
@@ -267,15 +268,17 @@ def tile_list_laureate_shortlist_page_kernel(
                 page[c][:].indirect(idx3[:, hf * LIST_COLS : (hf + 1) * LIST_COLS]), y[:], wgo_sb[hf][:], ALU.mult,
             )
 
-        second_feature(0, kept([P, PACK, HALF], F32, "best0"))
+        second_feature(0, kept([P, PACK, HALF], F32, "w1_raw0"))
         w1_q.append(quantize_weight(w1_raw[1], "w1q1", P))
         first_feature(0)
-        w3_q = [quantize_weight(w3_raw[0], "w3q0", 0), quantize_weight(w3_raw[1], "w3q1", VECTOR_SHARE)]
-        features(0, nc.vector.tensor_copy)
+        w3_q.append(quantize_weight(w3_raw[1], "w3q1", 0))
+        features(0, nc.scalar.copy)
+        v2_sc = kept([P, S2], U8, "v2_sc")
+        nc.vector.tensor_copy(v2_sc[:], tab2_sc[:].indirect(idx2[:]))
         v2_w = kept([P, S2], U32, "v2_w")
         nc.vector.tensor_copy(v2_w[:], tab2_w[:].indirect(idx2[:]))
         second_feature(1, kept([P, PACK, HALF], F32, "w3_raw1"))
-        first_feature(1)
+        first_feature(1, kept([P, PACK, HALF], F32, "w1_raw0"))
         scores(0, 0, on_vector=True)
         scores(1, 0)
         features(1, nc.scalar.copy)

@@ -26,7 +26,7 @@ HALF = 512
 HALVES = S // HALF
 LIST_COLS = HALF // 16
 ROW_TILES = S2 // P
-VECTOR_SHARE = 80
+WEAVE_SHARE = 40
 
 
 def tile_list_laureate_shortlist_page_kernel(
@@ -58,13 +58,15 @@ def tile_list_laureate_shortlist_page_kernel(
             nc.sync.dma_start(out=raw[:], in_=w[a * K_PASS : (a + 1) * K_PASS, :].rearrange("(p j) c -> p j c", j=PACK))
             return raw
 
-        tab_sc = kept([P, PASSES * T], U8, "tab_sc")
-        nc.vector.memset(tab_sc[:, :T].bitcast(I32), 0)
-        nc.gpsimd.memset(tab_sc[:, T:].bitcast(I32), 0)
         w2_sc_raw = kept([P, PASSES * H], U8, "w2_sc_raw")
+        nc.vector.memset(w2_sc_raw[:].bitcast(I32), 0)
+        tab_sc = kept([P, T], U8, "tab_sc")
+        nc.vector.memset(tab_sc[32:64, :].bitcast(I32), 0)
+        nc.vector.memset(tab_sc[64:128, :].bitcast(I32), 0)
+        v_sc = kept([P, PASSES * S], U8, "v_sc")
         tab2_sc = kept([P, T3], U8, "tab2_sc")
         w4_sc = kept([P, PASSES * S2], U8, "w4_sc")
-        for tile in (w2_sc_raw, tab2_sc, w4_sc):
+        for tile in (v_sc, tab2_sc, w4_sc):
             nc.vector.memset(tile[:].bitcast(I32), 0)
         ident = kept([P, P], F32, "ident")
         make_identity(nc, ident[:])
@@ -73,31 +75,39 @@ def tile_list_laureate_shortlist_page_kernel(
         idx2 = kept([P, S2 // 16], U16, "idx2")
         idx3 = kept([P, S // 16], U16, "idx3")
         nc.sync.dma_start(idx[:], offs)
+        nc.sync.dma_start(out=tab_sc[0:32, :].bitcast(I32), in_=tab_scales.rearrange("a q t -> q a t").bitcast(I32))
+        tab_w = [kept([P, T], U32, f"tab_w{a}") for a in range(PASSES)]
+        load_words(tab_w[0], tab_words[0])
+        w2_raw = kept([P, PASSES * 2 * H], U8, "w2_raw")
+        nc.sync.dma_start(
+            out=w2_raw[:].bitcast(I32).rearrange("p (a c) -> p a c", a=PASSES),
+            in_=w2_words.rearrange("a p c -> p a c").bitcast(I32),
+        )
+        load_scale_rows(w2_sc_raw, w2_scales)
+        w1_raw = [load_weight(w1, 0, "w1_raw0")]
+        w3_raw = [load_weight(w3, 0, "w3_raw0")]
+        load_words(tab_w[1], tab_words[1])
+
+        picked_sc = kept([P, S], U8, "picked_sc")
+        nc.vector.tensor_copy(picked_sc[:], tab_sc[:].indirect(idx[:]))
+        for q in range(QUADS):
+            nc.scalar.dma_start(
+                out=v_sc[32 * q : 32 * q + 4, :].bitcast(I32), in_=picked_sc[8 * q : 8 * q + 8, :].bitcast(I32)
+            )
+
+        w1_raw.append(load_weight(w1, 1, "w1_raw1"))
+        w3_raw.append(load_weight(w3, 1, "w3_raw1"))
         nc.sync.dma_start(idx2[:], offs2)
-        nc.sync.dma_start(idx3[:], offs3)
         b_sb = kept([P, PACK], F32, "b_sb")
         nc.sync.dma_start(out=b_sb[:], in_=b.rearrange("(p t) -> p t", t=PACK))
         gain_sb = kept([P, PACK], F32, "gain_sb")
         nc.sync.dma_start(out=gain_sb[:], in_=gain.rearrange("(p t) -> p t", t=PACK))
-        w2_raw = kept([P, PASSES * 2 * H], U8, "w2_raw")
-        for a in range(PASSES):
-            nc.sync.dma_start(out=w2_raw[:, 2 * H * a : 2 * H * (a + 1)].bitcast(I32), in_=w2_words[a].bitcast(I32))
-        tab_w = [kept([P, T], U32, f"tab_w{a}") for a in range(PASSES)]
-        load_words(tab_w[0], tab_words[0])
-        load_scale_rows(tab_sc, tab_scales)
-        w1_raw = [load_weight(w1, 0, "w1_raw0")]
-        load_scale_rows(w2_sc_raw, w2_scales)
-        w3_raw = [load_weight(w3, 0, "w3_raw0")]
-        load_words(tab_w[1], tab_words[1])
-        w1_raw.append(load_weight(w1, 1, "w1_raw1"))
-        w3_raw.append(load_weight(w3, 1, "w3_raw1"))
         d_sb = kept([P, ROW_TILES], F32, "d_sb")
         with nc.allow_non_contiguous_dma(reason="one value of d for each partition and row tile"):
             nc.sync.dma_start(out=d_sb[:], in_=d.rearrange("(c p) -> p c", p=P))
-        load_scale_rows(tab2_sc, tab2_scales)
         tab2_w = kept([P, T3], U32, "tab2_w")
         load_words(tab2_w, tab2_words[0])
-        load_scale_rows(w4_sc, w4_scales)
+        load_scale_rows(tab2_sc, tab2_scales)
         w4_w = kept([P, PASSES * S2], U32, "w4_w")
         nc.sync.dma_start(
             out=w4_w[:].bitcast(I32).rearrange("p (a c) -> p a c", a=PASSES),
@@ -119,9 +129,15 @@ def tile_list_laureate_shortlist_page_kernel(
             nc.sync.dma_start(out=page[c][:], in_=page1[c * P : (c + 1) * P, :])
 
         load_wgo(0)
-        for c in range(ROW_TILES):
-            load_jury(c, 0)
+        load_page(0)
+        load_scale_rows(w4_sc, w4_scales)
+        load_jury(0, 0)
+        nc.sync.dma_start(idx3[:], offs3)
+        load_page(1)
+        load_jury(1, 0)
+        for c in range(2, ROW_TILES):
             load_page(c)
+            load_jury(c, 0)
         load_wgo(1)
         for c in range(ROW_TILES):
             load_jury(c, 1)
@@ -133,10 +149,7 @@ def tile_list_laureate_shortlist_page_kernel(
         )
 
         v_w = [kept([P, S], U32, f"v_w{a}") for a in range(PASSES)]
-        v_sc = [kept([P, S], U8, f"v_sc{a}") for a in range(PASSES)]
         nc.vector.tensor_copy(v_w[0][:], tab_w[0][:].indirect(idx[:]))
-        for a in range(PASSES):
-            nc.vector.tensor_copy(v_sc[a][:], tab_sc[:, a * T : (a + 1) * T].indirect(idx[:]))
 
         w2_sc = kept([P, PASSES * H], U8, "w2_sc")
         nc.vector.tensor_copy(
@@ -172,7 +185,7 @@ def tile_list_laureate_shortlist_page_kernel(
                 lhs, lhs_sc = stationary[a]
                 nc.tensor.matmul_mx(
                     out=acc[:], lhsT=lhs, lhsT_scale=lhs_sc,
-                    rhs=v_w[a][:, cols].bitcast(FP8X4), rhs_scale=v_sc[a][:, cols],
+                    rhs=v_w[a][:, cols].bitcast(FP8X4), rhs_scale=v_sc[:, a * S + hf * HALF : a * S + (hf + 1) * HALF],
                     start=start and a == 0, stop=stop and a == PASSES - 1,
                 )
 
@@ -206,22 +219,23 @@ def tile_list_laureate_shortlist_page_kernel(
 
         h_q = {}
 
-        def features(hf, weave):
+        def features(hf, split):
             planes = ring.tile([P, PACK * HALF], BF16, name="planes", align_bytes=64)
             for t in range(PACK):
                 acc = psum.tile([P, HALF], F32, name="bank_c")
                 product(acc, columns(w3_q, t), hf)
-                th = ring.tile([P, HALF], F32, name="th", bufs=3)
+                th = ring.tile([P, HALF], F32, name="th", bufs=4)
                 nc.scalar.activation(out=th[:], in_=acc[:], func=ACT.Tanh, bias=b_sb[:, t : t + 1])
                 nc.vector.scalar_tensor_tensor(
                     out=planes[:, t * HALF : (t + 1) * HALF], in0=th[:], scalar=gain_sb[:, t : t + 1],
                     in1=best[hf, t], op0=ALU.mult, op1=ALU.add,
                 )
             woven = ring.tile([P, HALF * PACK], BF16, name="woven", align_bytes=64)
-            weave(
-                out=woven[:].rearrange("p (c i t) -> p c t i", i=4, t=PACK),
-                in_=planes[:].rearrange("p (t c i) -> p c t i", t=PACK, i=4),
-            )
+            dst = woven[:].rearrange("p (c i t) -> p c t i", i=4, t=PACK)
+            src = planes[:].rearrange("p (t c i) -> p c t i", t=PACK, i=4)
+            if split:
+                nc.vector.tensor_copy(out=dst[:, :split], in_=src[:, :split])
+            nc.scalar.copy(out=dst[:, split:], in_=src[:, split:])
             codes = kept([P, HALF], U32, f"h_w{hf}")
             scales = kept([P, HALF], U8, f"h_sc{hf}")
             nc.vector.quantize_mx(out=codes[:].bitcast(FP8X4), scales=scales[:], in_=woven[:])
@@ -272,7 +286,7 @@ def tile_list_laureate_shortlist_page_kernel(
         w1_q.append(quantize_weight(w1_raw[1], "w1q1", P))
         first_feature(0)
         w3_q.append(quantize_weight(w3_raw[1], "w3q1", 0))
-        features(0, nc.scalar.copy)
+        features(0, 0)
         v2_sc = kept([P, S2], U8, "v2_sc")
         nc.vector.tensor_copy(v2_sc[:], tab2_sc[:].indirect(idx2[:]))
         v2_w = kept([P, S2], U32, "v2_w")
@@ -281,7 +295,7 @@ def tile_list_laureate_shortlist_page_kernel(
         first_feature(1, kept([P, PACK, HALF], F32, "w1_raw0"))
         scores(0, 0, on_vector=True)
         scores(1, 0)
-        features(1, nc.scalar.copy)
+        features(1, 0)
         scores(2, 0)
         scores(3, 0)
         for c in range(ROW_TILES):

@@ -76,6 +76,7 @@ def tile_list_laureate_shortlist_page_kernel(
         idx3 = kept([P, S // 16], U16, "idx3")
         nc.sync.dma_start(idx[:], offs)
         nc.sync.dma_start(out=tab_sc[0:32, :].bitcast(I32), in_=tab_scales.rearrange("a q t -> q a t").bitcast(I32))
+        load_scale_rows(w2_sc_raw, w2_scales)
         tab_w = [kept([P, T], U32, f"tab_w{a}") for a in range(PASSES)]
         load_words(tab_w[0], tab_words[0])
         w2_raw = kept([P, PASSES * 2 * H], U8, "w2_raw")
@@ -83,9 +84,9 @@ def tile_list_laureate_shortlist_page_kernel(
             out=w2_raw[:].bitcast(I32).rearrange("p (a c) -> p a c", a=PASSES),
             in_=w2_words.rearrange("a p c -> p a c").bitcast(I32),
         )
-        load_scale_rows(w2_sc_raw, w2_scales)
         w1_raw = [load_weight(w1, 0, "w1_raw0")]
         w3_raw = [load_weight(w3, 0, "w3_raw0")]
+        nc.sync.dma_start(idx2[:], offs2)
         load_words(tab_w[1], tab_words[1])
 
         picked_sc = kept([P, S], U8, "picked_sc")
@@ -96,18 +97,18 @@ def tile_list_laureate_shortlist_page_kernel(
             )
 
         w1_raw.append(load_weight(w1, 1, "w1_raw1"))
-        w3_raw.append(load_weight(w3, 1, "w3_raw1"))
-        nc.sync.dma_start(idx2[:], offs2)
         b_sb = kept([P, PACK], F32, "b_sb")
         nc.sync.dma_start(out=b_sb[:], in_=b.rearrange("(p t) -> p t", t=PACK))
         gain_sb = kept([P, PACK], F32, "gain_sb")
         nc.sync.dma_start(out=gain_sb[:], in_=gain.rearrange("(p t) -> p t", t=PACK))
+        w3_raw.append(load_weight(w3, 1, "w3_raw1"))
         d_sb = kept([P, ROW_TILES], F32, "d_sb")
         with nc.allow_non_contiguous_dma(reason="one value of d for each partition and row tile"):
             nc.sync.dma_start(out=d_sb[:], in_=d.rearrange("(c p) -> p c", p=P))
+        load_scale_rows(tab2_sc, tab2_scales)
         tab2_w = kept([P, T3], U32, "tab2_w")
         load_words(tab2_w, tab2_words[0])
-        load_scale_rows(tab2_sc, tab2_scales)
+        load_scale_rows(w4_sc, w4_scales)
         w4_w = kept([P, PASSES * S2], U32, "w4_w")
         nc.sync.dma_start(
             out=w4_w[:].bitcast(I32).rearrange("p (a c) -> p a c", a=PASSES),
@@ -129,15 +130,12 @@ def tile_list_laureate_shortlist_page_kernel(
             nc.sync.dma_start(out=page[c][:], in_=page1[c * P : (c + 1) * P, :])
 
         load_wgo(0)
-        load_page(0)
-        load_scale_rows(w4_sc, w4_scales)
         load_jury(0, 0)
+        load_page(0)
         nc.sync.dma_start(idx3[:], offs3)
-        load_page(1)
-        load_jury(1, 0)
-        for c in range(2, ROW_TILES):
-            load_page(c)
+        for c in range(1, ROW_TILES):
             load_jury(c, 0)
+            load_page(c)
         load_wgo(1)
         for c in range(ROW_TILES):
             load_jury(c, 1)

@@ -85,9 +85,9 @@ def tile_list_laureate_shortlist_page_kernel(
             in_=w2_words.rearrange("a p c -> p a c").bitcast(I32),
         )
         w1_raw = [load_weight(w1, 0, "w1_raw0")]
-        w3_raw = [load_weight(w3, 0, "w3_raw0")]
-        nc.sync.dma_start(idx2[:], offs2)
         load_words(tab_w[1], tab_words[1])
+        nc.sync.dma_start(idx2[:], offs2)
+        w1_raw.append(load_weight(w1, 1, "w1_raw1"))
 
         picked_sc = kept([P, S], U8, "picked_sc")
         nc.vector.tensor_copy(picked_sc[:], tab_sc[:].indirect(idx[:]))
@@ -96,7 +96,7 @@ def tile_list_laureate_shortlist_page_kernel(
                 out=v_sc[32 * q : 32 * q + 4, :].bitcast(I32), in_=picked_sc[8 * q : 8 * q + 8, :].bitcast(I32)
             )
 
-        w1_raw.append(load_weight(w1, 1, "w1_raw1"))
+        w3_raw = [load_weight(w3, 0, "w3_raw0")]
         b_sb = kept([P, PACK], F32, "b_sb")
         nc.sync.dma_start(out=b_sb[:], in_=b.rearrange("(p t) -> p t", t=PACK))
         gain_sb = kept([P, PACK], F32, "gain_sb")
@@ -169,7 +169,6 @@ def tile_list_laureate_shortlist_page_kernel(
             return codes, scales
 
         w1_q = [quantize_weight(w1_raw[0], "w1q0", 0)]
-        w3_q = [quantize_weight(w3_raw[0], "w3q0", 0)]
 
         for hf in range(HALVES):
             nc.vector.tensor_copy(
@@ -283,7 +282,7 @@ def tile_list_laureate_shortlist_page_kernel(
         second_feature(0, kept([P, PACK, HALF], F32, "w1_raw0"))
         w1_q.append(quantize_weight(w1_raw[1], "w1q1", P))
         first_feature(0)
-        w3_q.append(quantize_weight(w3_raw[1], "w3q1", 0))
+        w3_q = [quantize_weight(w3_raw[a], f"w3q{a}", 0) for a in range(PASSES)]
         features(0, 0)
         v2_sc = kept([P, S2], U8, "v2_sc")
         nc.vector.tensor_copy(v2_sc[:], tab2_sc[:].indirect(idx2[:]))

from contextlib import ExitStack

import concourse.mybir as mybir
from concourse.masks import make_identity

K, T, S, H, S2, T3, T2 = 1024, 4096, 1024, 512, 512, 2048, 2048
FLOPS = 2 * S * (3 * K * H + H * S2 + K * S2)

F32 = mybir.dt.float32
BF16 = mybir.dt.bfloat16
I32 = mybir.dt.int32
U32 = mybir.dt.uint32
U16 = mybir.dt.uint16
U8 = mybir.dt.uint8
FP8X4 = mybir.dt.float8_e4m3fn_x4
FP4X4 = mybir.dt.float4_e2m1fn_x4
ALU = mybir.AluOpType
ACT = mybir.ActivationFunctionType

P = 128
PACK = 4
K_PASS = P * PACK
PASSES = K // K_PASS
QUADS = 4
HALF = 512
HALVES = S // HALF
LIST_COLS = HALF // 16
ROW_TILES = S2 // P
WEAVE_SHARE = 40


def tile_list_laureate_shortlist_page_kernel(
    tc, tab_words, tab_scales, tab2_words, tab2_scales, offs, offs2, offs3, w1, w2_words, w2_scales,
    w3, b, gain, w4_words, w4_scales, d, jury, page1, wgo, out,
):
    nc = tc.nc
    with ExitStack() as ctx:
        keep = ctx.enter_context(tc.tile_pool(name="keep", bufs=1))
        ring = ctx.enter_context(tc.tile_pool(name="ring", bufs=2))
        psum = ctx.enter_context(tc.psum_pool(name="psum", bufs=2))

        def kept(shape, dtype, name):
            return keep.tile(shape, dtype, name=name, align_bytes=64)

        def load_scale_rows(tile, src):
            passes = src.shape[0]
            for q in range(QUADS):
                nc.sync.dma_start(
                    out=tile[32 * q : 32 * q + 4, :].bitcast(I32).rearrange("r (a c) -> r a c", a=passes),
                    in_=src[:, 4 * q : 4 * q + 4, :].rearrange("a r c -> r a c").bitcast(I32),
                )

        def load_words(tile, src):
            nc.sync.dma_start(out=tile[:].bitcast(I32), in_=src.rearrange("p t i -> p (t i)").bitcast(I32))

        def load_weight(w, a, name):
            raw = kept([P, PACK, H], F32, name)
            nc.sync.dma_start(out=raw[:], in_=w[a * K_PASS : (a + 1) * K_PASS, :].rearrange("(p j) c -> p j c", j=PACK))
            return raw

        w2_sc_raw = kept([P, PASSES * H], U8, "w2_sc_raw")
        nc.vector.memset(w2_sc_raw[:].bitcast(I32), 0)
        tab_sc = kept([P, T], U8, "tab_sc")
        nc.vector.memset(tab_sc[32:64, :].bitcast(I32), 0)
        nc.vector.memset(tab_sc[64:128, :].bitcast(I32), 0)
        v_sc = kept([P, PASSES * S], U8, "v_sc")
        tab2_sc = kept([P, T3], U8, "tab2_sc")
        w4_sc = kept([P, PASSES * S2], U8, "w4_sc")
        for tile in (v_sc, tab2_sc, w4_sc):
            nc.vector.memset(tile[:].bitcast(I32), 0)
        ident = kept([P, P], F32, "ident")
        make_identity(nc, ident[:])

        idx = kept([P, S // 16], U16, "idx")
        idx2 = kept([P, S2 // 16], U16, "idx2")
        idx3 = kept([P, S // 16], U16, "idx3")
        nc.sync.dma_start(idx[:], offs)
        nc.sync.dma_start(out=tab_sc[0:32, :].bitcast(I32), in_=tab_scales.rearrange("a q t -> q a t").bitcast(I32))
        load_scale_rows(w2_sc_raw, w2_scales)
        tab_w = [kept([P, T], U32, f"tab_w{a}") for a in range(PASSES)]
        load_words(tab_w[0], tab_words[0])
        w2_raw = kept([P, PASSES * 2 * H], U8, "w2_raw")
        nc.sync.dma_start(
            out=w2_raw[:].bitcast(I32).rearrange("p (a c) -> p a c", a=PASSES),
            in_=w2_words.rearrange("a p c -> p a c").bitcast(I32),
        )
        w1_raw = [load_weight(w1, 0, "w1_raw0")]
        load_words(tab_w[1], tab_words[1])
        nc.sync.dma_start(idx2[:], offs2)
        w1_raw.append(load_weight(w1, 1, "w1_raw1"))

        picked_sc = kept([P, S], U8, "picked_sc")
        nc.vector.tensor_copy(picked_sc[:], tab_sc[:].indirect(idx[:]))
        for q in range(QUADS):
            nc.scalar.dma_start(
                out=v_sc[32 * q : 32 * q + 4, :].bitcast(I32), in_=picked_sc[8 * q : 8 * q + 8, :].bitcast(I32)
            )

        w3_raw = [load_weight(w3, 0, "w3_raw0")]
        b_sb = kept([P, PACK], F32, "b_sb")
        nc.sync.dma_start(out=b_sb[:], in_=b.rearrange("(p t) -> p t", t=PACK))
        gain_sb = kept([P, PACK], F32, "gain_sb")
        nc.sync.dma_start(out=gain_sb[:], in_=gain.rearrange("(p t) -> p t", t=PACK))
        w3_raw.append(load_weight(w3, 1, "w3_raw1"))
        d_sb = kept([P, ROW_TILES], F32, "d_sb")
        with nc.allow_non_contiguous_dma(reason="one value of d for each partition and row tile"):
            nc.sync.dma_start(out=d_sb[:], in_=d.rearrange("(c p) -> p c", p=P))
        load_scale_rows(tab2_sc, tab2_scales)
        tab2_w = kept([P, T3], U32, "tab2_w")
        load_words(tab2_w, tab2_words[0])
        load_scale_rows(w4_sc, w4_scales)
        w4_w = kept([P, PASSES * S2], U32, "w4_w")
        nc.sync.dma_start(
            out=w4_w[:].bitcast(I32).rearrange("p (a c) -> p a c", a=PASSES),
            in_=w4_words.rearrange("a p c i -> p a (c i)").bitcast(I32),
        )

        wgo_sb, jury_sb, page = {}, {}, {}

        def load_wgo(hf):
            wgo_sb[hf] = kept([P, HALF], F32, f"wgo{hf}")
            nc.sync.dma_start(out=wgo_sb[hf][:], in_=wgo[:, hf * HALF : (hf + 1) * HALF])

        def load_jury(c, hf):
            jury_sb[c, hf] = kept([P, HALF], F32, f"jury{c}_{hf}")
            nc.sync.dma_start(out=jury_sb[c, hf][:], in_=jury[c * P : (c + 1) * P, hf * HALF : (hf + 1) * HALF])

        def load_page(c):
            page[c] = kept([P, T2], F32, f"page{c}")
            nc.sync.dma_start(out=page[c][:], in_=page1[c * P : (c + 1) * P, :])

        load_wgo(0)
        load_jury(0, 0)
        load_page(0)
        nc.sync.dma_start(idx3[:], offs3)
        for c in range(1, ROW_TILES):
            load_jury(c, 0)
            load_page(c)
        load_wgo(1)
        for c in range(ROW_TILES):
            load_jury(c, 1)

        w2_w = kept([P, PASSES * 2 * H], U8, "w2_w")
        nc.vector.tensor_copy(
            out=w2_w[:].bitcast(U16).rearrange("p (a t m) -> p a t m", a=PASSES, t=PACK),
            in_=w2_raw[:].bitcast(U16).rearrange("p (a m t) -> p a t m", a=PASSES, t=PACK),
        )

        v_w = [kept([P, S], U32, f"v_w{a}") for a in range(PASSES)]
        nc.vector.tensor_copy(v_w[0][:], tab_w[0][:].indirect(idx[:]))

        w2_sc = kept([P, PASSES * H], U8, "w2_sc")
        nc.vector.tensor_copy(
            out=w2_sc[:].rearrange("p (a t m) -> p a t m", a=PASSES, t=PACK),
            in_=w2_sc_raw[:].rearrange("p (a m t) -> p a t m", a=PASSES, t=PACK),
        )

        def quantize_weight(raw, name, split):
            grouped = ring.tile([P, PACK * H], BF16, name="grouped", align_bytes=64)
            dst = grouped[:].rearrange("p (t m j) -> p m j t", t=PACK, j=PACK)
            src = raw[:].rearrange("p j (m t) -> p m j t", t=PACK)
            if split:
                nc.vector.tensor_copy(out=dst[:, :split], in_=src[:, :split])
            if split < P:
                nc.scalar.copy(out=dst[:, split:], in_=src[:, split:])
            codes = kept([P, H], U32, name + "_w")
            scales = kept([P, H], U8, name + "_sc")
            nc.vector.quantize_mx(out=codes[:].bitcast(FP8X4), scales=scales[:], in_=grouped[:])
            return codes, scales

        w1_q = [quantize_weight(w1_raw[0], "w1q0", 0)]

        for hf in range(HALVES):
            nc.vector.tensor_copy(
                v_w[1][:, hf * HALF : (hf + 1) * HALF],
                tab_w[1][:].indirect(idx[:, hf * LIST_COLS : (hf + 1) * LIST_COLS]),
            )

        def product(acc, stationary, hf, start=True, stop=True):
            cols = slice(hf * HALF, (hf + 1) * HALF)
            for a in range(PASSES):
                lhs, lhs_sc = stationary[a]
                nc.tensor.matmul_mx(
                    out=acc[:], lhsT=lhs, lhsT_scale=lhs_sc,
                    rhs=v_w[a][:, cols].bitcast(FP8X4), rhs_scale=v_sc[:, a * S + hf * HALF : a * S + (hf + 1) * HALF],
                    start=start and a == 0, stop=stop and a == PASSES - 1,
                )

        def columns(q, t):
            return [(codes[:, t * P : (t + 1) * P].bitcast(FP8X4), scales[:, t * P : (t + 1) * P]) for codes, scales in q]

        best = {}

        def second_feature(hf, store):
            for t in range(PACK):
                acc = psum.tile([P, HALF], F32, name="bank_a")
                stationary = [
                    (
                        w2_w[:, 2 * (a * H + t * P) : 2 * (a * H + (t + 1) * P)].bitcast(FP4X4),
                        w2_sc[:, a * H + t * P : a * H + (t + 1) * P],
                    )
                    for a in range(PASSES)
                ]
                product(acc, stationary, hf)
                best[hf, t] = store[:, t, :]
                nc.scalar.copy(out=best[hf, t], in_=acc[:])

        def first_feature(hf, store=None):
            for t in range(PACK):
                acc = psum.tile([P, HALF], F32, name="bank_b")
                product(acc, columns(w1_q, t), hf)
                f2 = best[hf, t]
                if store is not None:
                    best[hf, t] = store[:, t, :]
                nc.vector.tensor_tensor(out=best[hf, t], in0=acc[:], in1=f2, op=ALU.max)

        h_q = {}

        def features(hf, split):
            planes = ring.tile([P, PACK * HALF], BF16, name="planes", align_bytes=64)
            for t in range(PACK):
                acc = psum.tile([P, HALF], F32, name="bank_c")
                product(acc, columns(w3_q, t), hf)
                th = ring.tile([P, HALF], F32, name="th", bufs=4)
                nc.scalar.activation(out=th[:], in_=acc[:], func=ACT.Tanh, bias=b_sb[:, t : t + 1])
                nc.vector.scalar_tensor_tensor(
                    out=planes[:, t * HALF : (t + 1) * HALF], in0=th[:], scalar=gain_sb[:, t : t + 1],
                    in1=best[hf, t], op0=ALU.mult, op1=ALU.add,
                )
            woven = ring.tile([P, HALF * PACK], BF16, name="woven", align_bytes=64)
            dst = woven[:].rearrange("p (c i t) -> p c t i", i=4, t=PACK)
            src = planes[:].rearrange("p (t c i) -> p c t i", t=PACK, i=4)
            if split:
                nc.vector.tensor_copy(out=dst[:, :split], in_=src[:, :split])
            nc.scalar.copy(out=dst[:, split:], in_=src[:, split:])
            codes = kept([P, HALF], U32, f"h_w{hf}")
            scales = kept([P, HALF], U8, f"h_sc{hf}")
            nc.vector.quantize_mx(out=codes[:].bitcast(FP8X4), scales=scales[:], in_=woven[:])
            h_q[hf] = codes, scales

        def scores(c, hf, on_vector=False):
            acc = psum.tile([P, HALF], F32, name="e")
            stationary = [
                (
                    w4_w[:, a * S2 + c * P : a * S2 + (c + 1) * P].bitcast(FP8X4),
                    w4_sc[:, a * S2 + c * P : a * S2 + (c + 1) * P],
                )
                for a in range(PASSES)
            ]
            product(acc, stationary, hf, stop=False)
            codes, scales = h_q[hf]
            nc.tensor.matmul_mx(
                out=acc[:], lhsT=v2_w[:, c * P : (c + 1) * P].bitcast(FP8X4), lhsT_scale=v2_sc[:, c * P : (c + 1) * P],
                rhs=codes[:].bitcast(FP8X4), rhs_scale=scales[:], start=False, stop=True,
            )
            y = ring.tile([P, HALF], F32, name="y", bufs=3)
            if on_vector:
                nc.vector.scalar_tensor_tensor(
                    out=y[:], in0=acc[:], scalar=d_sb[:, c : c + 1], in1=jury_sb[c, hf][:], op0=ALU.mult, op1=ALU.add,
                )
            else:
                z = ring.tile([P, HALF], F32, name="z")
                nc.scalar.activation(out=z[:], in_=acc[:], func=ACT.Copy, scale=d_sb[:, c : c + 1])
                turned = psum.tile([P, HALF], F32, name="bank_a")
                blocks = [slice(i * P, (i + 1) * P) for i in range(HALF // P)]
                for n, term in enumerate((jury_sb[c, hf], z)):
                    for i, blk in enumerate(blocks):
                        nc.tensor.matmul(
                            turned[:, blk], term[:, blk], ident[:], is_transpose=True,
                            start=(n == 0 and i == 0), stop=(n == 1 and i == len(blocks) - 1),
                        )
                y_t = ring.tile([P, HALF], F32, name="y_t")
                nc.scalar.copy(out=y_t[:], in_=turned[:])
                back = psum.tile([P, HALF], F32, name="bank_b")
                for blk in blocks:
                    nc.tensor.transpose(back[:, blk], y_t[:, blk], ident[:])
                nc.scalar.copy(out=y[:], in_=back[:])
            nc.vector.tensor_tensor(
                page[c][:].indirect(idx3[:, hf * LIST_COLS : (hf + 1) * LIST_COLS]), y[:], wgo_sb[hf][:], ALU.mult,
            )

        second_feature(0, kept([P, PACK, HALF], F32, "w1_raw0"))
        w1_q.append(quantize_weight(w1_raw[1], "w1q1", P))
        first_feature(0)
        w3_q = [quantize_weight(w3_raw[a], f"w3q{a}", 0) for a in range(PASSES)]
        features(0, 0)
        v2_sc = kept([P, S2], U8, "v2_sc")
        nc.vector.tensor_copy(v2_sc[:], tab2_sc[:].indirect(idx2[:]))
        v2_w = kept([P, S2], U32, "v2_w")
        nc.vector.tensor_copy(v2_w[:], tab2_w[:].indirect(idx2[:]))
        second_feature(1, kept([P, PACK, HALF], F32, "w3_raw1"))
        first_feature(1, kept([P, PACK, HALF], F32, "w1_raw0"))
        scores(0, 0, on_vector=True)
        scores(1, 0)
        features(1, 0)
        scores(2, 0)
        scores(3, 0)
        for c in range(ROW_TILES):
            scores(c, 1)
            nc.sync.dma_start(out=out[c * P : (c + 1) * P, :], in_=page[c][:])
